import numpy as np
import ml_dtypes


def mxq(x, axis, fmt="e4m3"):
    dtype, down = {"e4m3": (ml_dtypes.float8_e4m3fn, 7), "e5m2": (ml_dtypes.float8_e5m2, 14)}[fmt]
    v = np.moveaxis(np.asarray(x, np.float32).astype(ml_dtypes.bfloat16).astype(np.float64), axis, -1)
    blocks = v.reshape(v.shape[:-1] + (-1, 32))
    amax = np.abs(blocks).max(-1, keepdims=True)
    byte = np.maximum(np.where(amax > 0, np.frexp(amax)[1] - 1 + 127, 0) - down, 1)
    scale = np.exp2(byte - 127.0)
    codes = (blocks / scale).astype(np.float32).astype(dtype).astype(np.float64)
    return np.moveaxis((codes * scale).reshape(v.shape), -1, axis)


WIDE = False


def mx_kscale(k):
    if not WIDE:
        return np.ones(k)
    levels = np.array([10, -10, 5, -5, 0])
    if k % 512:
        return np.exp2(np.random.permutation(np.resize(levels, k // 32))).repeat(32)
    a = np.empty((k // 512, 16))
    for p in range(k // 512):
        a[p, :8] = np.random.permutation(np.resize(levels, 8))
        for g in range(8):
            far = levels[np.abs(levels - a[p, g]) >= 10]
            a[p, g + 8] = far[np.random.randint(len(far))]
    return np.exp2(a.ravel()).repeat(32)


BF16 = ml_dtypes.bfloat16


def bf(x):
    return np.asarray(x, np.float32).astype(BF16)


def f64(x):
    return np.asarray(x).astype(np.float64)


E2M1 = np.array([0.0, 0.5, 1.0, 1.5, 2.0, 3.0, 4.0, 6.0, -0.0, -0.5, -1.0, -1.5, -2.0, -3.0, -4.0, -6.0])


def pack_weight(w, fmt):
    k, n = w.shape
    w = f64(bf(w)).reshape(k // 32, 32, n)
    amax = np.abs(w).max(1)
    if fmt == "e4m3":
        byte = np.frexp(amax)[1] - 1 + 127 - 7
    else:
        mant, ex = np.frexp(amax / 6.0)
        byte = np.where(mant > 0.5, ex, ex - 1) + 127
    byte = np.clip(np.where(amax > 0, byte, 1), 1, 254)
    scaled = (w * np.exp2(127.0 - byte)[:, None, :]).reshape(k, n).astype(np.float32)
    by_word = np.ascontiguousarray(scaled.reshape(k // 512, 128, 4, n).transpose(0, 1, 3, 2))
    if fmt == "e4m3":
        words = by_word.astype(ml_dtypes.float8_e4m3fn).view(np.uint8)
    else:
        c = by_word.astype(ml_dtypes.float4_e2m1fn).view(np.uint8) & 0xF
        words = c[..., 0::2] | (c[..., 1::2] << 4)
    return np.ascontiguousarray(words), np.ascontiguousarray(byte.astype(np.uint8).reshape(k // 512, 16, n))


def unpack_weight(words, scales, fmt):
    g, p, n, _ = words.shape
    if fmt == "e4m3":
        vals = np.ascontiguousarray(words).view(ml_dtypes.float8_e4m3fn).astype(np.float64)
    else:
        nib = np.empty((g, p, n, 4), np.uint8)
        nib[..., 0::2] = words & 0xF
        nib[..., 1::2] = words >> 4
        vals = E2M1[nib]
    vals = vals * np.repeat(np.exp2(scales.astype(np.float64) - 127.0), 8, axis=1)[..., None]
    return vals.transpose(0, 1, 3, 2).reshape(g * 512, n)
def pack4(w):
    words, scales = pack_weight(w, "e2m1")
    return words.reshape(words.shape[0], 128, -1), scales


def unpack4(words, scales):
    return unpack_weight(words.reshape(words.shape[0], 128, -1, 2), scales, "e2m1")


def planes(Y):
    n, m = Y.shape
    b = f64(bf(Y)).reshape(n // 32, 32, m)
    amax = np.abs(b).max(1)
    byte = np.clip(np.where(amax > 0, np.frexp(amax)[1] - 1 + 127 - 7, 1), 1, 254)
    codes = (b * np.exp2(127.0 - byte)[:, None, :]).reshape(n, m).astype(np.float32).astype(ml_dtypes.float8_e4m3fn).view(np.uint8)
    words = codes.reshape(n // 512, 128, 4, m).transpose(0, 1, 3, 2)
    return np.ascontiguousarray(words), np.ascontiguousarray(byte.astype(np.uint8).reshape(n // 512, 16, m))


DIM, PROBES = 1024, 1536

def symmetric(d, size):
    r = np.random.randn(DIM, DIM)
    return size * d[:, None] * d[None, :] * (r + r.T) / np.sqrt(2 * DIM)

def setup_inputs():
    s = mx_kscale(DIM)
    d = np.exp(0.3 * np.random.randn(DIM))
    b, e, u = symmetric(d, 0.75), symmetric(d, 0.45), symmetric(d, 0.45)
    v = np.where(np.random.randn(PROBES, DIM) > 0, 1.0, -1.0)
    a32, v32 = (b + e + u).astype(np.float32), v.T.astype(np.float32)
    z = np.zeros((DIM, PROBES), np.float32)
    for j in range(DIM):
        z += a32[:, j, None] * v32[j]
    c = np.exp(0.8 * np.random.randn(PROBES))
    c = c / np.mean(c)
    z_words, z_scales = pack_weight(f64(z) * s[:, None], "e4m3")
    b_words, b_scales = pack4(b / s[:, None])
    e_words, e_scales = pack_weight(e / s[:, None], "e4m3")
    return {"z_words": z_words, "z_scales": z_scales, "b_words": b_words, "b_scales": b_scales,
            "e_words": e_words, "e_scales": e_scales, "u": bf(u / s[:, None]), "v": bf(v), "c": bf(c)}

def reference(z_words, z_scales, b_words, b_scales, e_words, e_scales, u, v, c):
    z = unpack_weight(z_words, z_scales, "e4m3")
    b = unpack4(b_words, b_scales)
    e = unpack_weight(e_words, e_scales, "e4m3")
    uq = mxq(f64(u), 0, "e4m3")
    pb = z.T @ b
    pe = z.T @ e
    pu = z.T @ uq
    y = f64(c)[:, None] * (f64(v) * (pb + pe + pu))
    words, scales = planes(y)
    return y, words, scales

@@ -1,0 +1,284 @@
+from contextlib import ExitStack
+
+import concourse.mybir as mybir
+
+DIM, PROBES = 1024, 1536
+FLOPS = 3 * 2 * DIM * PROBES * DIM
+
+F32 = mybir.dt.float32
+BF16 = mybir.dt.bfloat16
+I32 = mybir.dt.int32
+U8 = mybir.dt.uint8
+FP8X4 = mybir.dt.float8_e4m3fn_x4
+FP4X4 = mybir.dt.float4_e2m1fn_x4
+MULT = mybir.AluOpType.mult
+
+P = 128
+PACK = 4
+GROUP = P * PACK
+PASSES = DIM // GROUP
+GROUPS = PROBES // GROUP
+WIDE = 512
+NARROW = 128
+HALVES = DIM // WIDE
+QUADS = 4
+
+
+def tile_hutchinson_diagonal_probe_samples_k3_kernel(
+    tc, z_words, z_scales, b_words, b_scales, e_words, e_scales, u, v, c, out_0, out_1, out_2
+):
+    nc = tc.nc
+    with ExitStack() as ctx:
+        keep = ctx.enter_context(tc.tile_pool(name="keep", bufs=1))
+        work = ctx.enter_context(tc.tile_pool(name="work", bufs=3))
+        psum = ctx.enter_context(tc.psum_pool(name="psum", bufs=1))
+        ctx.enter_context(tc.manual_schedule())
+
+        def kept(name, shape, dtype):
+            return keep.tile(shape, dtype, name=name, align_bytes=64)
+
+        z_rows = z_words.rearrange("k p n t -> p k (n t)")
+        e_rows = e_words.rearrange("k p n t -> k p (n t)")
+
+        zs_first = kept("zs_first", [P, PASSES, GROUP], U8)
+        zs_rest = kept("zs_rest", [P, PASSES, PROBES - GROUP], U8)
+        bs = kept("bs", [P, PASSES, DIM], U8)
+        es = kept("es", [P, PASSES, DIM], U8)
+        for plane in (zs_first, bs, es, zs_rest):
+            nc.vector.memset(plane[:].bitcast(I32), 0)
+
+        def load_scale_rows(queue, plane, scales, quad):
+            queue.dma_start(
+                out=plane[32 * quad : 32 * quad + 4, :, :].bitcast(I32),
+                in_=scales[:, 4 * quad : 4 * quad + 4, :].rearrange("k r n -> r k n").bitcast(I32),
+            )
+
+        z_raw = {}
+
+        def load_z(g, k):
+            z_raw[g, k] = kept("z_raw_%d_%d" % (g, k), [P, GROUP], I32)
+            nc.sync.dma_start(
+                out=z_raw[g, k][:], in_=z_rows[:, k, PACK * GROUP * g : PACK * GROUP * (g + 1)].bitcast(I32)
+            )
+
+        bw, ew, u_raw, v_sb = {}, {}, {}, {}
+
+        def load_b(k):
+            bw[k] = kept("bw_%d" % k, [P, 2 * DIM], U8)
+            nc.sync.dma_start(out=bw[k][:].bitcast(I32), in_=b_words[k].bitcast(I32))
+
+        def load_e(k):
+            ew[k] = kept("ew_%d" % k, [P, DIM], I32)
+            nc.sync.dma_start(out=ew[k][:], in_=e_rows[k].bitcast(I32))
+
+        def load_u(h, k):
+            u_raw[h, k] = kept("u_raw_%d_%d" % (h, k), [P, PACK, WIDE], BF16)
+            rows = u[GROUP * k : GROUP * (k + 1), WIDE * h : WIDE * (h + 1)]
+            nc.sync.dma_start(out=u_raw[h, k][:], in_=rows.rearrange("(p j) n -> p j n", j=PACK))
+
+        def load_v(g, h):
+            v_sb[g, h] = kept("v_%d_%d" % (g, h), [P, PACK, WIDE], BF16)
+            rows = v[GROUP * g : GROUP * (g + 1), WIDE * h : WIDE * (h + 1)]
+            nc.sync.dma_start(out=v_sb[g, h][:], in_=rows.rearrange("(p t) n -> p t n", t=PACK))
+
+        for quad in range(QUADS):
+            load_scale_rows(nc.sync, zs_first, z_scales[:, :, :GROUP], quad)
+        load_z(0, 0)
+        load_b(0)
+        for quad in range(QUADS):
+            load_scale_rows(nc.sync, bs, b_scales, quad)
+        load_z(0, 1)
+        load_b(1)
+        for quad in range(QUADS):
+            load_scale_rows(nc.sync, es, e_scales, quad)
+        load_u(0, 0)
+        load_e(0)
+        load_u(0, 1)
+        load_e(1)
+        load_u(1, 0)
+        load_u(1, 1)
+        for quad in range(QUADS):
+            load_scale_rows(nc.sync, zs_rest, z_scales[:, :, GROUP:], quad)
+        load_z(1, 0)
+        load_z(1, 1)
+        c_sb = kept("c_sb", [P, GROUPS, PACK], BF16)
+        nc.sync.dma_start(out=c_sb[:], in_=c.rearrange("(g p t) -> p g t", p=P, t=PACK))
+        load_v(0, 0)
+        load_v(0, 1)
+        load_v(1, 0)
+        load_z(2, 0)
+        load_z(2, 1)
+        load_v(1, 1)
+        load_v(2, 0)
+        load_v(2, 1)
+
+        zw, zs = {}, {}
+
+        def sort_z(g, k):
+            zw[g, k] = kept("zw_%d_%d" % (g, k), [P, GROUP], I32)
+            zs[g, k] = kept("zs_%d_%d" % (g, k), [P, GROUP], U8)
+            nc.vector.tensor_copy(
+                out=zw[g, k][:].rearrange("p (t a i) -> p a t i", t=PACK, i=4),
+                in_=z_raw[g, k][:].rearrange("p (a i t) -> p a t i", t=PACK, i=4),
+            )
+            raw = zs_first[:, k, :] if g == 0 else zs_rest[:, k, GROUP * (g - 1) : GROUP * g]
+            nc.vector.tensor_copy(
+                out=zs[g, k][:].rearrange("p (t a i) -> p a t i", t=PACK, i=16),
+                in_=raw.rearrange("p (a i t) -> p a t i", t=PACK, i=16),
+            )
+
+        def interleave(copy, dst, src):
+            copy(
+                out=dst.rearrange("p (a i) t -> p a t i", i=4),
+                in_=src.rearrange("p t (a i) -> p a t i", i=4),
+            )
+
+        u_side, uw, us = {}, {}, {}
+
+        def interleave_u(h, k):
+            u_side[h, k] = kept("u_side_%d_%d" % (h, k), [P, WIDE, PACK], BF16)
+            interleave(nc.scalar.copy if k == 0 else nc.vector.tensor_copy, u_side[h, k][:], u_raw[h, k][:])
+
+        def quantise_u(h, k):
+            uw[h, k] = kept("uw_%d_%d" % (h, k), [P, WIDE], I32)
+            us[h, k] = kept("us_%d_%d" % (h, k), [P, WIDE], U8)
+            nc.vector.quantize_mx(
+                out=uw[h, k][:].bitcast(FP8X4), scales=us[h, k][:], in_=u_side[h, k][:].rearrange("p n j -> p (n j)")
+            )
+
+        def one_pass(acc, part, k, g, t, col, width):
+            cols = slice(col, col + width)
+            if part == "b":
+                rhs, rhs_scale = bw[k][:, 2 * col : 2 * (col + width)].bitcast(FP4X4), bs[:, k, cols]
+            elif part == "e":
+                rhs, rhs_scale = ew[k][:, cols].bitcast(FP8X4), es[:, k, cols]
+            else:
+                h, inner = divmod(col, WIDE)
+                rhs = uw[h, k][:, inner : inner + width].bitcast(FP8X4)
+                rhs_scale = us[h, k][:, inner : inner + width]
+            nc.tensor.matmul_mx(
+                out=acc[:, :width],
+                lhsT=zw[g, k][:, P * t : P * (t + 1)].bitcast(FP8X4),
+                lhsT_scale=zs[g, k][:, P * t : P * (t + 1)],
+                rhs=rhs,
+                rhs_scale=rhs_scale,
+                start=(part == "b" and k == 0),
+                stop=(part == "u" and k == PASSES - 1),
+            )
+
+        def bank(n):
+            return psum.tile([P, WIDE], F32, name="bank_%d" % n)
+
+        y_scales = [kept("y_scales_%d" % g, [P, DIM], U8) for g in range(GROUPS)]
+        y_words = [kept("y_words_%d" % g, [P, DIM], I32) for g in range(GROUPS)]
+        waiting = []
+
+        def store_scales(g, cols, queues):
+            for quad in range(QUADS):
+                queues[quad % len(queues)].dma_start(
+                    out=out_2[g, 4 * quad : 4 * quad + 4, cols].bitcast(I32),
+                    in_=y_scales[g][32 * quad : 32 * quad + 4, cols].bitcast(I32),
+                )
+
+        def store_words(g, col, end):
+            words = out_1[g].rearrange("p m t -> p (m t)")[:, PACK * col : PACK * end]
+            nc.sync.dma_start(out=words.bitcast(I32), in_=y_words[g][:, col:end])
+
+        def quantise_y(g, col, width, side):
+            nc.vector.quantize_mx(
+                out=y_words[g][:, col : col + width].bitcast(FP8X4),
+                scales=y_scales[g][:, col : col + width],
+                in_=side[:, :width, :].rearrange("p n t -> p (n t)"),
+            )
+            end = col + width
+            if width == WIDE or end == DIM:
+                store_words(g, col, end)
+            elif end == DIM - NARROW:
+                store_words(g, WIDE, end)
+            if end == DIM:
+                store_scales(g, slice(0, DIM), [nc.sync] if g < GROUPS - 1 else [nc.scalar, nc.sync])
+
+        def weigh(dst, acc, g, t, col, width):
+            h, inner = divmod(col, WIDE)
+            nc.vector.scalar_tensor_tensor(
+                out=dst,
+                in0=acc[:, :width],
+                scalar=c_sb[:, g, t : t + 1],
+                in1=v_sb[g, h][:, t, inner : inner + width],
+                op0=MULT,
+                op1=MULT,
+            )
+
+        def empty_bank(acc, y, g, t, col, width):
+            weigh(y[:, t, :width], acc, g, t, col, width)
+            for entry in waiting:
+                entry[0] = entry[0] - width
+            if waiting and waiting[0][0] <= 0:
+                oldest = waiting[0]
+                waiting.remove(oldest)
+                quantise_y(*oldest[1:])
+
+        def finish_block(y, g, col, width):
+            rows = out_0[GROUP * g : GROUP * (g + 1), col : col + width]
+            nc.sync.dma_start(out=rows.rearrange("(p t) n -> p t n", t=PACK), in_=y[:, :, :width])
+            side = work.tile([P, WIDE, PACK], BF16, name="side", align_bytes=64)
+            interleave(nc.scalar.copy, side[:, :width, :], y[:, :, :width])
+            waiting.append([2 * width, g, col, width, side])
+
+        def y_tile():
+            return work.tile([P, PACK, WIDE], F32, name="y", align_bytes=64)
+
+        for k in range(PASSES):
+            sort_z(0, k)
+        for h in range(HALVES):
+            for k in range(PASSES):
+                interleave_u(h, k)
+            for k in range(PASSES):
+                quantise_u(h, k)
+        for k in range(PASSES):
+            sort_z(1, k)
+
+        banks = [bank(n) for n in range(HALVES * PACK)]
+        for part in ("b", "e"):
+            for k in range(PASSES):
+                for h in range(HALVES):
+                    for t in range(PACK):
+                        one_pass(banks[PACK * h + t], part, k, 0, t, WIDE * h, WIDE)
+        for h in range(HALVES):
+            y = y_tile()
+            for t in range(PACK):
+                for k in range(PASSES):
+                    one_pass(banks[PACK * h + t], "u", k, 0, t, WIDE * h, WIDE)
+                empty_bank(banks[PACK * h + t], y, 0, t, WIDE * h, WIDE)
+            finish_block(y, 0, WIDE * h, WIDE)
+
+        blocks = [(1, 0, WIDE), (1, WIDE, WIDE), (2, 0, WIDE)]
+        blocks = blocks + [(2, col, NARROW) for col in range(WIDE, DIM - NARROW, NARROW)]
+        for n, (g, col, width) in enumerate(blocks):
+            y = y_tile()
+            for t in range(PACK):
+                acc = bank(PACK * (n % 2) + t)
+                for part in ("b", "e", "u"):
+                    for k in range(PASSES):
+                        one_pass(acc, part, k, g, t, col, width)
+                empty_bank(acc, y, g, t, col, width)
+            finish_block(y, g, col, width)
+            if n == 0:
+                for k in range(PASSES):
+                    sort_z(2, k)
+
+        g, col, width = GROUPS - 1, DIM - NARROW, NARROW
+        y = y_tile()
+        side = work.tile([P, WIDE, PACK], BF16, name="side", align_bytes=64)
+        rows = out_0[GROUP * g :, col:].rearrange("(p t) n -> p t n", t=PACK)
+        for t in range(PACK):
+            acc = bank(PACK * (len(blocks) % 2) + t)
+            for part in ("b", "e", "u"):
+                for k in range(PASSES):
+                    one_pass(acc, part, k, g, t, col, width)
+            empty_bank(acc, y, g, t, col, width)
+            if t == 2:
+                nc.sync.dma_start(out=rows[:, :3, :], in_=y[:, :3, :width])
+        nc.sync.dma_start(out=rows[:, 3, :], in_=y[:, 3, :width])
+        interleave(nc.vector.tensor_copy, side[:, :width, :], y[:, :, :width])
+        quantise_y(g, col, width, side)

@@ -19,7 +19,9 @@ GROUP = P * PACK
 PASSES = DIM // GROUP
 GROUPS = PROBES // GROUP
 WIDE = 512
+MIDDLE = 256
 NARROW = 128
+WARM_PASSES = 20
 HALVES = DIM // WIDE
 QUADS = 4
 
@@ -44,8 +46,30 @@ def tile_hutchinson_diagonal_probe_samples_k3_kernel(
         zs_rest = kept("zs_rest", [P, PASSES, PROBES - GROUP], U8)
         bs = kept("bs", [P, PASSES, DIM], U8)
         es = kept("es", [P, PASSES, DIM], U8)
-        for plane in (zs_first, bs, es, zs_rest):
-            nc.vector.memset(plane[:].bitcast(I32), 0)
+
+        def bank(n):
+            return psum.tile([P, WIDE], F32, name="bank_%d" % n)
+
+        ones = kept("ones", [P, PACK * NARROW], BF16)
+        ones_words = kept("ones_words", [P, NARROW], I32)
+        ones_scales = kept("ones_scales", [P, NARROW], U8)
+        nc.gpsimd.memset(zs_first[:].bitcast(I32), 0)
+        nc.vector.memset(ones[:], 1.0)
+        nc.vector.memset(bs[:].bitcast(I32), 0)
+        nc.vector.quantize_mx(out=ones_words[:].bitcast(FP8X4), scales=ones_scales[:], in_=ones[:])
+        nc.vector.memset(es[:].bitcast(I32), 0)
+        nc.vector.memset(zs_rest[:].bitcast(I32), 0)
+        idle = bank(HALVES * PACK - 1)
+        for n in range(WARM_PASSES):
+            nc.tensor.matmul_mx(
+                out=idle[:, :NARROW],
+                lhsT=ones_words[:].bitcast(FP8X4),
+                lhsT_scale=ones_scales[:],
+                rhs=ones_words[:].bitcast(FP8X4),
+                rhs_scale=ones_scales[:],
+                start=True,
+                stop=True,
+            )
 
         def load_scale_rows(queue, plane, scales, quad):
             queue.dma_start(
@@ -71,15 +95,15 @@ def tile_hutchinson_diagonal_probe_samples_k3_kernel(
             ew[k] = kept("ew_%d" % k, [P, DIM], I32)
             nc.sync.dma_start(out=ew[k][:], in_=e_rows[k].bitcast(I32))
 
-        def load_u(h, k):
-            u_raw[h, k] = kept("u_raw_%d_%d" % (h, k), [P, PACK, WIDE], BF16)
-            rows = u[GROUP * k : GROUP * (k + 1), WIDE * h : WIDE * (h + 1)]
-            nc.sync.dma_start(out=u_raw[h, k][:], in_=rows.rearrange("(p j) n -> p j n", j=PACK))
+        def load_u(k):
+            u_raw[k] = kept("u_raw_%d" % k, [P, PACK, DIM], BF16)
+            rows = u[GROUP * k : GROUP * (k + 1), :]
+            nc.sync.dma_start(out=u_raw[k][:], in_=rows.rearrange("(p j) n -> p j n", j=PACK))
 
-        def load_v(g, h):
-            v_sb[g, h] = kept("v_%d_%d" % (g, h), [P, PACK, WIDE], BF16)
-            rows = v[GROUP * g : GROUP * (g + 1), WIDE * h : WIDE * (h + 1)]
-            nc.sync.dma_start(out=v_sb[g, h][:], in_=rows.rearrange("(p t) n -> p t n", t=PACK))
+        def load_v(g):
+            v_sb[g] = kept("v_%d" % g, [P, PACK, DIM], BF16)
+            rows = v[GROUP * g : GROUP * (g + 1), :]
+            nc.sync.dma_start(out=v_sb[g][:], in_=rows.rearrange("(p t) n -> p t n", t=PACK))
 
         for quad in range(QUADS):
             load_scale_rows(nc.sync, zs_first, z_scales[:, :, :GROUP], quad)
@@ -91,26 +115,20 @@ def tile_hutchinson_diagonal_probe_samples_k3_kernel(
         load_b(1)
         for quad in range(QUADS):
             load_scale_rows(nc.sync, es, e_scales, quad)
-        load_u(0, 0)
-        load_e(0)
-        load_u(0, 1)
-        load_e(1)
-        load_u(1, 0)
-        load_u(1, 1)
+        for k in range(PASSES):
+            load_e(k)
+            load_u(k)
         for quad in range(QUADS):
             load_scale_rows(nc.sync, zs_rest, z_scales[:, :, GROUP:], quad)
         load_z(1, 0)
         load_z(1, 1)
         c_sb = kept("c_sb", [P, GROUPS, PACK], BF16)
         nc.sync.dma_start(out=c_sb[:], in_=c.rearrange("(g p t) -> p g t", p=P, t=PACK))
-        load_v(0, 0)
-        load_v(0, 1)
-        load_v(1, 0)
+        load_v(0)
+        load_v(1)
         load_z(2, 0)
         load_z(2, 1)
-        load_v(1, 1)
-        load_v(2, 0)
-        load_v(2, 1)
+        load_v(2)
 
         zw, zs = {}, {}
 
@@ -137,7 +155,8 @@ def tile_hutchinson_diagonal_probe_samples_k3_kernel(
 
         def interleave_u(h, k):
             u_side[h, k] = kept("u_side_%d_%d" % (h, k), [P, WIDE, PACK], BF16)
-            interleave(nc.scalar.copy if k == 0 else nc.vector.tensor_copy, u_side[h, k][:], u_raw[h, k][:])
+            copy = nc.scalar.copy if h == 1 else nc.vector.tensor_copy
+            interleave(copy, u_side[h, k][:], u_raw[k][:, :, WIDE * h : WIDE * (h + 1)])
 
         def quantise_u(h, k):
             uw[h, k] = kept("uw_%d_%d" % (h, k), [P, WIDE], I32)
@@ -146,7 +165,11 @@ def tile_hutchinson_diagonal_probe_samples_k3_kernel(
                 out=uw[h, k][:].bitcast(FP8X4), scales=us[h, k][:], in_=u_side[h, k][:].rearrange("p n j -> p (n j)")
             )
 
-        def one_pass(acc, part, k, g, t, col, width):
+        def one_pass(acc, part, k, g, t, col, width, first):
+            if part == "b" and width == MIDDLE:
+                for inner in range(0, MIDDLE, NARROW):
+                    one_pass(acc[:, inner:], part, k, g, t, col + inner, NARROW, first)
+                return
             cols = slice(col, col + width)
             if part == "b":
                 rhs, rhs_scale = bw[k][:, 2 * col : 2 * (col + width)].bitcast(FP4X4), bs[:, k, cols]
@@ -162,12 +185,9 @@ def tile_hutchinson_diagonal_probe_samples_k3_kernel(
                 lhsT_scale=zs[g, k][:, P * t : P * (t + 1)],
                 rhs=rhs,
                 rhs_scale=rhs_scale,
-                start=(part == "b" and k == 0),
+                start=(part == first and k == 0),
                 stop=(part == "u" and k == PASSES - 1),
             )
-
-        def bank(n):
-            return psum.tile([P, WIDE], F32, name="bank_%d" % n)
 
         y_scales = [kept("y_scales_%d" % g, [P, DIM], U8) for g in range(GROUPS)]
         y_words = [kept("y_words_%d" % g, [P, DIM], I32) for g in range(GROUPS)]
@@ -199,12 +219,11 @@ def tile_hutchinson_diagonal_probe_samples_k3_kernel(
                 store_scales(g, slice(0, DIM), [nc.sync] if g < GROUPS - 1 else [nc.scalar, nc.sync])
 
         def weigh(dst, acc, g, t, col, width):
-            h, inner = divmod(col, WIDE)
             nc.vector.scalar_tensor_tensor(
                 out=dst,
                 in0=acc[:, :width],
                 scalar=c_sb[:, g, t : t + 1],
-                in1=v_sb[g, h][:, t, inner : inner + width],
+                in1=v_sb[g][:, t, col : col + width],
                 op0=MULT,
                 op1=MULT,
             )
@@ -230,37 +249,35 @@ def tile_hutchinson_diagonal_probe_samples_k3_kernel(
 
         for k in range(PASSES):
             sort_z(0, k)
-        for h in range(HALVES):
-            for k in range(PASSES):
+        for k in range(PASSES):
+            for h in range(HALVES):
                 interleave_u(h, k)
-            for k in range(PASSES):
+            for h in range(HALVES):
                 quantise_u(h, k)
         for k in range(PASSES):
             sort_z(1, k)
 
         banks = [bank(n) for n in range(HALVES * PACK)]
-        for part in ("b", "e"):
-            for k in range(PASSES):
-                for h in range(HALVES):
-                    for t in range(PACK):
-                        one_pass(banks[PACK * h + t], part, k, 0, t, WIDE * h, WIDE)
+        for part, k in (("b", 0), ("b", 1), ("e", 0), ("e", 1), ("u", 0)):
+            for h in range(HALVES):
+                for t in range(PACK):
+                    one_pass(banks[PACK * h + t], part, k, 0, t, WIDE * h, WIDE, "b")
         for h in range(HALVES):
             y = y_tile()
             for t in range(PACK):
-                for k in range(PASSES):
-                    one_pass(banks[PACK * h + t], "u", k, 0, t, WIDE * h, WIDE)
+                one_pass(banks[PACK * h + t], "u", 1, 0, t, WIDE * h, WIDE, "b")
                 empty_bank(banks[PACK * h + t], y, 0, t, WIDE * h, WIDE)
             finish_block(y, 0, WIDE * h, WIDE)
 
         blocks = [(1, 0, WIDE), (1, WIDE, WIDE), (2, 0, WIDE)]
-        blocks = blocks + [(2, col, NARROW) for col in range(WIDE, DIM - NARROW, NARROW)]
+        blocks = blocks + [(2, WIDE, MIDDLE), (2, WIDE + MIDDLE, NARROW)]
         for n, (g, col, width) in enumerate(blocks):
             y = y_tile()
             for t in range(PACK):
                 acc = bank(PACK * (n % 2) + t)
-                for part in ("b", "e", "u"):
+                for part in ("e", "b", "u"):
                     for k in range(PASSES):
-                        one_pass(acc, part, k, g, t, col, width)
+                        one_pass(acc, part, k, g, t, col, width, "e")
                 empty_bank(acc, y, g, t, col, width)
             finish_block(y, g, col, width)
             if n == 0:
@@ -273,9 +290,9 @@ def tile_hutchinson_diagonal_probe_samples_k3_kernel(
         rows = out_0[GROUP * g :, col:].rearrange("(p t) n -> p t n", t=PACK)
         for t in range(PACK):
             acc = bank(PACK * (len(blocks) % 2) + t)
-            for part in ("b", "e", "u"):
+            for part in ("e", "b", "u"):
                 for k in range(PASSES):
-                    one_pass(acc, part, k, g, t, col, width)
+                    one_pass(acc, part, k, g, t, col, width, "e")
             empty_bank(acc, y, g, t, col, width)
             if t == 2:
                 nc.sync.dma_start(out=rows[:, :3, :], in_=y[:, :3, :width])

@@ -95,10 +95,12 @@ def tile_hutchinson_diagonal_probe_samples_k3_kernel(
             ew[k] = kept("ew_%d" % k, [P, DIM], I32)
             nc.sync.dma_start(out=ew[k][:], in_=e_rows[k].bitcast(I32))
 
-        def load_u(k):
-            u_raw[k] = kept("u_raw_%d" % k, [P, PACK, DIM], BF16)
-            rows = u[GROUP * k : GROUP * (k + 1), :]
-            nc.sync.dma_start(out=u_raw[k][:], in_=rows.rearrange("(p j) n -> p j n", j=PACK))
+        def load_u(k, col, width):
+            raw = kept("u_raw_%d_%d" % (k, col), [P, PACK, width], BF16)
+            rows = u[GROUP * k : GROUP * (k + 1), col : col + width]
+            nc.sync.dma_start(out=raw[:], in_=rows.rearrange("(p j) n -> p j n", j=PACK))
+            for inner in range(0, width, WIDE):
+                u_raw[(col + inner) // WIDE, k] = raw[:, :, inner : inner + WIDE]
 
         def load_v(g):
             v_sb[g] = kept("v_%d" % g, [P, PACK, DIM], BF16)
@@ -113,15 +115,17 @@ def tile_hutchinson_diagonal_probe_samples_k3_kernel(
             load_scale_rows(nc.sync, bs, b_scales, quad)
         load_z(0, 1)
         load_b(1)
+        load_e(0)
+        load_u(0, 0, WIDE)
         for quad in range(QUADS):
             load_scale_rows(nc.sync, es, e_scales, quad)
-        for k in range(PASSES):
-            load_e(k)
-            load_u(k)
-        for quad in range(QUADS):
-            load_scale_rows(nc.sync, zs_rest, z_scales[:, :, GROUP:], quad)
+        load_u(0, WIDE, WIDE)
+        load_e(1)
+        load_u(1, 0, DIM)
         load_z(1, 0)
         load_z(1, 1)
+        for quad in range(QUADS):
+            load_scale_rows(nc.sync, zs_rest, z_scales[:, :, GROUP:], quad)
         c_sb = kept("c_sb", [P, GROUPS, PACK], BF16)
         nc.sync.dma_start(out=c_sb[:], in_=c.rearrange("(g p t) -> p g t", p=P, t=PACK))
         load_v(0)
@@ -132,31 +136,34 @@ def tile_hutchinson_diagonal_probe_samples_k3_kernel(
 
         zw, zs = {}, {}
 
-        def sort_z(g, k):
+        def sort_words(g, k):
             zw[g, k] = kept("zw_%d_%d" % (g, k), [P, GROUP], I32)
-            zs[g, k] = kept("zs_%d_%d" % (g, k), [P, GROUP], U8)
             nc.vector.tensor_copy(
                 out=zw[g, k][:].rearrange("p (t a i) -> p a t i", t=PACK, i=4),
                 in_=z_raw[g, k][:].rearrange("p (a i t) -> p a t i", t=PACK, i=4),
             )
+
+        def sort_scales(g, k):
+            zs[g, k] = kept("zs_%d_%d" % (g, k), [P, GROUP], U8)
             raw = zs_first[:, k, :] if g == 0 else zs_rest[:, k, GROUP * (g - 1) : GROUP * g]
             nc.vector.tensor_copy(
                 out=zs[g, k][:].rearrange("p (t a i) -> p a t i", t=PACK, i=16),
                 in_=raw.rearrange("p (a i t) -> p a t i", t=PACK, i=16),
             )
 
+        def sort_z(g, k):
+            sort_words(g, k)
+            sort_scales(g, k)
+
         def interleave(copy, dst, src):
-            copy(
-                out=dst.rearrange("p (a i) t -> p a t i", i=4),
-                in_=src.rearrange("p t (a i) -> p a t i", i=4),
-            )
+            copy(out=dst, in_=src.rearrange("p t n -> p n t"))
 
         u_side, uw, us = {}, {}, {}
 
         def interleave_u(h, k):
             u_side[h, k] = kept("u_side_%d_%d" % (h, k), [P, WIDE, PACK], BF16)
-            copy = nc.scalar.copy if h == 1 else nc.vector.tensor_copy
-            interleave(copy, u_side[h, k][:], u_raw[k][:, :, WIDE * h : WIDE * (h + 1)])
+            copy = nc.scalar.copy if h == k else nc.vector.tensor_copy
+            interleave(copy, u_side[h, k][:], u_raw[h, k])
 
         def quantise_u(h, k):
             uw[h, k] = kept("uw_%d_%d" % (h, k), [P, WIDE], I32)
@@ -241,21 +248,27 @@ def tile_hutchinson_diagonal_probe_samples_k3_kernel(
             rows = out_0[GROUP * g : GROUP * (g + 1), col : col + width]
             nc.sync.dma_start(out=rows.rearrange("(p t) n -> p t n", t=PACK), in_=y[:, :, :width])
             side = work.tile([P, WIDE, PACK], BF16, name="side", align_bytes=64)
-            interleave(nc.scalar.copy, side[:, :width, :], y[:, :, :width])
+            share = max(NARROW, width // 2)
+            interleave(nc.scalar.copy, side[:, :share, :], y[:, :, :share])
+            if share < width:
+                interleave(nc.vector.tensor_copy, side[:, share:width, :], y[:, :, share:width])
             waiting.append([2 * width, g, col, width, side])
 
         def y_tile():
-            return work.tile([P, PACK, WIDE], F32, name="y", align_bytes=64)
+            return work.tile([P, PACK, WIDE], F32, name="y", bufs=4, align_bytes=64)
 
         for k in range(PASSES):
             sort_z(0, k)
         for k in range(PASSES):
             for h in range(HALVES):
                 interleave_u(h, k)
-            for h in range(HALVES):
-                quantise_u(h, k)
+            quantise_u(0, k)
+            if k == PASSES - 1:
+                for k_next in range(PASSES):
+                    sort_words(1, k_next)
+            quantise_u(1, k)
         for k in range(PASSES):
-            sort_z(1, k)
+            sort_scales(1, k)
 
         banks = [bank(n) for n in range(HALVES * PACK)]
         for part, k in (("b", 0), ("b", 1), ("e", 0), ("e", 1), ("u", 0)):

@@ -22,6 +22,7 @@ WIDE = 512
 MIDDLE = 256
 NARROW = 128
 WARM_PASSES = 20
+GROUP_ORDER = (("e", 0), ("u", 0), ("b", 0), ("b", 1), ("e", 1), ("u", 1))
 HALVES = DIM // WIDE
 QUADS = 4
 
@@ -37,7 +38,7 @@ def tile_hutchinson_diagonal_probe_samples_k3_kernel(
         ctx.enter_context(tc.manual_schedule())
 
         def kept(name, shape, dtype):
-            return keep.tile(shape, dtype, name=name, align_bytes=64)
+            return keep.tile(shape, dtype, name=name, align_bytes=256)
 
         z_rows = z_words.rearrange("k p n t -> p k (n t)")
         e_rows = e_words.rearrange("k p n t -> k p (n t)")
@@ -247,7 +248,7 @@ def tile_hutchinson_diagonal_probe_samples_k3_kernel(
         def finish_block(y, g, col, width):
             rows = out_0[GROUP * g : GROUP * (g + 1), col : col + width]
             nc.sync.dma_start(out=rows.rearrange("(p t) n -> p t n", t=PACK), in_=y[:, :, :width])
-            side = work.tile([P, WIDE, PACK], BF16, name="side", align_bytes=64)
+            side = work.tile([P, WIDE, PACK], BF16, name="side", align_bytes=256)
             share = max(NARROW, width // 2)
             interleave(nc.scalar.copy, side[:, :share, :], y[:, :, :share])
             if share < width:
@@ -255,7 +256,7 @@ def tile_hutchinson_diagonal_probe_samples_k3_kernel(
             waiting.append([2 * width, g, col, width, side])
 
         def y_tile():
-            return work.tile([P, PACK, WIDE], F32, name="y", bufs=4, align_bytes=64)
+            return work.tile([P, PACK, WIDE], F32, name="y", bufs=4, align_bytes=256)
 
         for k in range(PASSES):
             sort_z(0, k)
@@ -272,8 +273,8 @@ def tile_hutchinson_diagonal_probe_samples_k3_kernel(
 
         banks = [bank(n) for n in range(HALVES * PACK)]
         for part, k in (("b", 0), ("b", 1), ("e", 0), ("e", 1), ("u", 0)):
-            for h in range(HALVES):
-                for t in range(PACK):
+            for t in range(PACK):
+                for h in range(HALVES):
                     one_pass(banks[PACK * h + t], part, k, 0, t, WIDE * h, WIDE, "b")
         for h in range(HALVES):
             y = y_tile()
@@ -288,9 +289,8 @@ def tile_hutchinson_diagonal_probe_samples_k3_kernel(
             y = y_tile()
             for t in range(PACK):
                 acc = bank(PACK * (n % 2) + t)
-                for part in ("e", "b", "u"):
-                    for k in range(PASSES):
-                        one_pass(acc, part, k, g, t, col, width, "e")
+                for part, k in GROUP_ORDER:
+                    one_pass(acc, part, k, g, t, col, width, "e")
                 empty_bank(acc, y, g, t, col, width)
             finish_block(y, g, col, width)
             if n == 0:
@@ -299,13 +299,12 @@ def tile_hutchinson_diagonal_probe_samples_k3_kernel(
 
         g, col, width = GROUPS - 1, DIM - NARROW, NARROW
         y = y_tile()
-        side = work.tile([P, WIDE, PACK], BF16, name="side", align_bytes=64)
+        side = work.tile([P, WIDE, PACK], BF16, name="side", align_bytes=256)
         rows = out_0[GROUP * g :, col:].rearrange("(p t) n -> p t n", t=PACK)
         for t in range(PACK):
             acc = bank(PACK * (len(blocks) % 2) + t)
-            for part in ("e", "b", "u"):
-                for k in range(PASSES):
-                    one_pass(acc, part, k, g, t, col, width, "e")
+            for part, k in GROUP_ORDER:
+                one_pass(acc, part, k, g, t, col, width, "e")
             empty_bank(acc, y, g, t, col, width)
             if t == 2:
                 nc.sync.dma_start(out=rows[:, :3, :], in_=y[:, :3, :width])

from contextlib import ExitStack

import concourse.mybir as mybir

DIM, PROBES = 1024, 1536
FLOPS = 3 * 2 * DIM * PROBES * DIM

F32 = mybir.dt.float32
BF16 = mybir.dt.bfloat16
I32 = mybir.dt.int32
U8 = mybir.dt.uint8
FP8X4 = mybir.dt.float8_e4m3fn_x4
FP4X4 = mybir.dt.float4_e2m1fn_x4
MULT = mybir.AluOpType.mult

P = 128
PACK = 4
GROUP = P * PACK
PASSES = DIM // GROUP
GROUPS = PROBES // GROUP
WIDE = 512
MIDDLE = 256
NARROW = 128
WARM_PASSES = 20
GROUP_ORDER = (("e", 0), ("u", 0), ("b", 0), ("b", 1), ("e", 1), ("u", 1))
HALVES = DIM // WIDE
QUADS = 4


def tile_hutchinson_diagonal_probe_samples_k3_kernel(
    tc, z_words, z_scales, b_words, b_scales, e_words, e_scales, u, v, c, out_0, out_1, out_2
):
    nc = tc.nc
    with ExitStack() as ctx:
        keep = ctx.enter_context(tc.tile_pool(name="keep", bufs=1))
        work = ctx.enter_context(tc.tile_pool(name="work", bufs=3))
        psum = ctx.enter_context(tc.psum_pool(name="psum", bufs=1))
        ctx.enter_context(tc.manual_schedule())

        def kept(name, shape, dtype):
            return keep.tile(shape, dtype, name=name, align_bytes=256)

        z_rows = z_words.rearrange("k p n t -> p k (n t)")
        e_rows = e_words.rearrange("k p n t -> k p (n t)")

        zs_first = kept("zs_first", [P, PASSES, GROUP], U8)
        zs_rest = kept("zs_rest", [P, PASSES, PROBES - GROUP], U8)
        bs = kept("bs", [P, PASSES, DIM], U8)
        es = kept("es", [P, PASSES, DIM], U8)

        def bank(n):
            return psum.tile([P, WIDE], F32, name="bank_%d" % n)

        ones = kept("ones", [P, PACK * NARROW], BF16)
        ones_words = kept("ones_words", [P, NARROW], I32)
        ones_scales = kept("ones_scales", [P, NARROW], U8)
        nc.gpsimd.memset(zs_first[:].bitcast(I32), 0)
        nc.vector.memset(ones[:], 1.0)
        nc.vector.memset(bs[:].bitcast(I32), 0)
        nc.vector.quantize_mx(out=ones_words[:].bitcast(FP8X4), scales=ones_scales[:], in_=ones[:])
        nc.vector.memset(es[:].bitcast(I32), 0)
        nc.vector.memset(zs_rest[:].bitcast(I32), 0)
        idle = bank(HALVES * PACK - 1)
        for n in range(WARM_PASSES):
            nc.tensor.matmul_mx(
                out=idle[:, :NARROW],
                lhsT=ones_words[:].bitcast(FP8X4),
                lhsT_scale=ones_scales[:],
                rhs=ones_words[:].bitcast(FP8X4),
                rhs_scale=ones_scales[:],
                start=True,
                stop=True,
            )

        def load_scale_rows(queue, plane, scales, quad):
            queue.dma_start(
                out=plane[32 * quad : 32 * quad + 4, :, :].bitcast(I32),
                in_=scales[:, 4 * quad : 4 * quad + 4, :].rearrange("k r n -> r k n").bitcast(I32),
            )

        z_raw = {}

        def load_z(g, k):
            z_raw[g, k] = kept("z_raw_%d_%d" % (g, k), [P, GROUP], I32)
            nc.sync.dma_start(
                out=z_raw[g, k][:], in_=z_rows[:, k, PACK * GROUP * g : PACK * GROUP * (g + 1)].bitcast(I32)
            )

        bw, ew, u_raw, v_sb = {}, {}, {}, {}

        def load_b(k):
            bw[k] = kept("bw_%d" % k, [P, 2 * DIM], U8)
            nc.sync.dma_start(out=bw[k][:].bitcast(I32), in_=b_words[k].bitcast(I32))

        def load_e(k):
            ew[k] = kept("ew_%d" % k, [P, DIM], I32)
            nc.sync.dma_start(out=ew[k][:], in_=e_rows[k].bitcast(I32))

        def load_u(k, col, width):
            raw = kept("u_raw_%d_%d" % (k, col), [P, PACK, width], BF16)
            rows = u[GROUP * k : GROUP * (k + 1), col : col + width]
            nc.sync.dma_start(out=raw[:], in_=rows.rearrange("(p j) n -> p j n", j=PACK))
            for inner in range(0, width, WIDE):
                u_raw[(col + inner) // WIDE, k] = raw[:, :, inner : inner + WIDE]

        def load_v(g):
            v_sb[g] = kept("v_%d" % g, [P, PACK, DIM], BF16)
            rows = v[GROUP * g : GROUP * (g + 1), :]
            nc.sync.dma_start(out=v_sb[g][:], in_=rows.rearrange("(p t) n -> p t n", t=PACK))

        for quad in range(QUADS):
            load_scale_rows(nc.sync, zs_first, z_scales[:, :, :GROUP], quad)
        load_z(0, 0)
        load_b(0)
        for quad in range(QUADS):
            load_scale_rows(nc.sync, bs, b_scales, quad)
        load_z(0, 1)
        load_b(1)
        load_e(0)
        load_u(0, 0, WIDE)
        for quad in range(QUADS):
            load_scale_rows(nc.sync, es, e_scales, quad)
        load_u(0, WIDE, WIDE)
        load_e(1)
        load_u(1, 0, DIM)
        load_z(1, 0)
        load_z(1, 1)
        for quad in range(QUADS):
            load_scale_rows(nc.sync, zs_rest, z_scales[:, :, GROUP:], quad)
        c_sb = kept("c_sb", [P, GROUPS, PACK], BF16)
        nc.sync.dma_start(out=c_sb[:], in_=c.rearrange("(g p t) -> p g t", p=P, t=PACK))
        load_v(0)
        load_v(1)
        load_z(2, 0)
        load_z(2, 1)
        load_v(2)

        zw, zs = {}, {}

        def sort_words(g, k):
            zw[g, k] = kept("zw_%d_%d" % (g, k), [P, GROUP], I32)
            nc.vector.tensor_copy(
                out=zw[g, k][:].rearrange("p (t a i) -> p a t i", t=PACK, i=4),
                in_=z_raw[g, k][:].rearrange("p (a i t) -> p a t i", t=PACK, i=4),
            )

        def sort_scales(g, k):
            zs[g, k] = kept("zs_%d_%d" % (g, k), [P, GROUP], U8)
            raw = zs_first[:, k, :] if g == 0 else zs_rest[:, k, GROUP * (g - 1) : GROUP * g]
            nc.vector.tensor_copy(
                out=zs[g, k][:].rearrange("p (t a i) -> p a t i", t=PACK, i=16),
                in_=raw.rearrange("p (a i t) -> p a t i", t=PACK, i=16),
            )

        def sort_z(g, k):
            sort_words(g, k)
            sort_scales(g, k)

        def interleave(copy, dst, src):
            copy(out=dst, in_=src.rearrange("p t n -> p n t"))

        u_side, uw, us = {}, {}, {}

        def interleave_u(h, k):
            u_side[h, k] = kept("u_side_%d_%d" % (h, k), [P, WIDE, PACK], BF16)
            copy = nc.scalar.copy if h == k else nc.vector.tensor_copy
            interleave(copy, u_side[h, k][:], u_raw[h, k])

        def quantise_u(h, k):
            uw[h, k] = kept("uw_%d_%d" % (h, k), [P, WIDE], I32)
            us[h, k] = kept("us_%d_%d" % (h, k), [P, WIDE], U8)
            nc.vector.quantize_mx(
                out=uw[h, k][:].bitcast(FP8X4), scales=us[h, k][:], in_=u_side[h, k][:].rearrange("p n j -> p (n j)")
            )

        def one_pass(acc, part, k, g, t, col, width, first):
            if part == "b" and width == MIDDLE:
                for inner in range(0, MIDDLE, NARROW):
                    one_pass(acc[:, inner:], part, k, g, t, col + inner, NARROW, first)
                return
            cols = slice(col, col + width)
            if part == "b":
                rhs, rhs_scale = bw[k][:, 2 * col : 2 * (col + width)].bitcast(FP4X4), bs[:, k, cols]
            elif part == "e":
                rhs, rhs_scale = ew[k][:, cols].bitcast(FP8X4), es[:, k, cols]
            else:
                h, inner = divmod(col, WIDE)
                rhs = uw[h, k][:, inner : inner + width].bitcast(FP8X4)
                rhs_scale = us[h, k][:, inner : inner + width]
            nc.tensor.matmul_mx(
                out=acc[:, :width],
                lhsT=zw[g, k][:, P * t : P * (t + 1)].bitcast(FP8X4),
                lhsT_scale=zs[g, k][:, P * t : P * (t + 1)],
                rhs=rhs,
                rhs_scale=rhs_scale,
                start=(part == first and k == 0),
                stop=(part == "u" and k == PASSES - 1),
            )

        y_scales = [kept("y_scales_%d" % g, [P, DIM], U8) for g in range(GROUPS)]
        y_words = [kept("y_words_%d" % g, [P, DIM], I32) for g in range(GROUPS)]
        waiting = []

        def store_scales(g, cols, queues):
            for quad in range(QUADS):
                queues[quad % len(queues)].dma_start(
                    out=out_2[g, 4 * quad : 4 * quad + 4, cols].bitcast(I32),
                    in_=y_scales[g][32 * quad : 32 * quad + 4, cols].bitcast(I32),
                )

        def store_words(g, col, end):
            words = out_1[g].rearrange("p m t -> p (m t)")[:, PACK * col : PACK * end]
            nc.sync.dma_start(out=words.bitcast(I32), in_=y_words[g][:, col:end])

        def quantise_y(g, col, width, side):
            nc.vector.quantize_mx(
                out=y_words[g][:, col : col + width].bitcast(FP8X4),
                scales=y_scales[g][:, col : col + width],
                in_=side[:, :width, :].rearrange("p n t -> p (n t)"),
            )
            end = col + width
            if width == WIDE or end == DIM:
                store_words(g, col, end)
            elif end == DIM - NARROW:
                store_words(g, WIDE, end)
            if end == DIM:
                store_scales(g, slice(0, DIM), [nc.sync] if g < GROUPS - 1 else [nc.scalar, nc.sync])

        def weigh(dst, acc, g, t, col, width):
            nc.vector.scalar_tensor_tensor(
                out=dst,
                in0=acc[:, :width],
                scalar=c_sb[:, g, t : t + 1],
                in1=v_sb[g][:, t, col : col + width],
                op0=MULT,
                op1=MULT,
            )

        def empty_bank(acc, y, g, t, col, width):
            weigh(y[:, t, :width], acc, g, t, col, width)
            for entry in waiting:
                entry[0] = entry[0] - width
            if waiting and waiting[0][0] <= 0:
                oldest = waiting[0]
                waiting.remove(oldest)
                quantise_y(*oldest[1:])

        def finish_block(y, g, col, width):
            rows = out_0[GROUP * g : GROUP * (g + 1), col : col + width]
            nc.sync.dma_start(out=rows.rearrange("(p t) n -> p t n", t=PACK), in_=y[:, :, :width])
            side = work.tile([P, WIDE, PACK], BF16, name="side", align_bytes=256)
            share = max(NARROW, width // 2)
            interleave(nc.scalar.copy, side[:, :share, :], y[:, :, :share])
            if share < width:
                interleave(nc.vector.tensor_copy, side[:, share:width, :], y[:, :, share:width])
            waiting.append([2 * width, g, col, width, side])

        def y_tile():
            return work.tile([P, PACK, WIDE], F32, name="y", bufs=4, align_bytes=256)

        for k in range(PASSES):
            sort_z(0, k)
        for k in range(PASSES):
            for h in range(HALVES):
                interleave_u(h, k)
            quantise_u(0, k)
            if k == PASSES - 1:
                for k_next in range(PASSES):
                    sort_words(1, k_next)
            quantise_u(1, k)
        for k in range(PASSES):
            sort_scales(1, k)

        banks = [bank(n) for n in range(HALVES * PACK)]
        for part, k in (("b", 0), ("b", 1), ("e", 0), ("e", 1), ("u", 0)):
            for t in range(PACK):
                for h in range(HALVES):
                    one_pass(banks[PACK * h + t], part, k, 0, t, WIDE * h, WIDE, "b")
        for h in range(HALVES):
            y = y_tile()
            for t in range(PACK):
                one_pass(banks[PACK * h + t], "u", 1, 0, t, WIDE * h, WIDE, "b")
                empty_bank(banks[PACK * h + t], y, 0, t, WIDE * h, WIDE)
            finish_block(y, 0, WIDE * h, WIDE)

        blocks = [(1, 0, WIDE), (1, WIDE, WIDE), (2, 0, WIDE)]
        blocks = blocks + [(2, WIDE, MIDDLE), (2, WIDE + MIDDLE, NARROW)]
        for n, (g, col, width) in enumerate(blocks):
            y = y_tile()
            for t in range(PACK):
                acc = bank(PACK * (n % 2) + t)
                for part, k in GROUP_ORDER:
                    one_pass(acc, part, k, g, t, col, width, "e")
                empty_bank(acc, y, g, t, col, width)
            finish_block(y, g, col, width)
            if n == 0:
                for k in range(PASSES):
                    sort_z(2, k)

        g, col, width = GROUPS - 1, DIM - NARROW, NARROW
        y = y_tile()
        side = work.tile([P, WIDE, PACK], BF16, name="side", align_bytes=256)
        rows = out_0[GROUP * g :, col:].rearrange("(p t) n -> p t n", t=PACK)
        for t in range(PACK):
            acc = bank(PACK * (len(blocks) % 2) + t)
            for part, k in GROUP_ORDER:
                one_pass(acc, part, k, g, t, col, width, "e")
            empty_bank(acc, y, g, t, col, width)
            if t == 2:
                nc.sync.dma_start(out=rows[:, :3, :], in_=y[:, :3, :width])
        nc.sync.dma_start(out=rows[:, 3, :], in_=y[:, 3, :width])
        interleave(nc.vector.tensor_copy, side[:, :width, :], y[:, :, :width])
        quantise_y(g, col, width, side)
